import numpy as np
import ml_dtypes


def mxq(x, axis, fmt="e4m3"):
    dtype, down = {"e4m3": (ml_dtypes.float8_e4m3fn, 7), "e5m2": (ml_dtypes.float8_e5m2, 14)}[fmt]
    v = np.moveaxis(np.asarray(x, np.float32).astype(ml_dtypes.bfloat16).astype(np.float64), axis, -1)
    blocks = v.reshape(v.shape[:-1] + (-1, 32))
    amax = np.abs(blocks).max(-1, keepdims=True)
    byte = np.maximum(np.where(amax > 0, np.frexp(amax)[1] - 1 + 127, 0) - down, 1)
    scale = np.exp2(byte - 127.0)
    codes = (blocks / scale).astype(np.float32).astype(dtype).astype(np.float64)
    return np.moveaxis((codes * scale).reshape(v.shape), -1, axis)


WIDE = False


def mx_kscale(k):
    if not WIDE:
        return np.ones(k)
    levels = np.array([10, -10, 5, -5, 0])
    if k % 512:
        return np.exp2(np.random.permutation(np.resize(levels, k // 32))).repeat(32)
    a = np.empty((k // 512, 16))
    for p in range(k // 512):
        a[p, :8] = np.random.permutation(np.resize(levels, 8))
        for g in range(8):
            far = levels[np.abs(levels - a[p, g]) >= 10]
            a[p, g + 8] = far[np.random.randint(len(far))]
    return np.exp2(a.ravel()).repeat(32)


def f64(x):
    return np.asarray(x).astype(np.float64)


def striped(idx):
    return np.tile(idx.reshape(-1, 16).T, (8, 1)).astype(np.uint16)


def unstriped(offs):
    return offs[:16].T.reshape(-1).astype(np.int64)


E2M1 = np.array([0.0, 0.5, 1.0, 1.5, 2.0, 3.0, 4.0, 6.0, -0.0, -0.5, -1.0, -1.5, -2.0, -3.0, -4.0, -6.0])


def pack_weight(w, fmt):
    k, n = w.shape
    w = f64(np.asarray(w, np.float32).astype(ml_dtypes.bfloat16)).reshape(k // 32, 32, n)
    amax = np.abs(w).max(1)
    if fmt == "e4m3":
        byte = np.frexp(amax)[1] - 1 + 127 - 7
    else:
        mant, ex = np.frexp(amax / 6.0)
        byte = np.where(mant > 0.5, ex, ex - 1) + 127
    byte = np.clip(np.where(amax > 0, byte, 1), 1, 254)
    scaled = (w * np.exp2(127.0 - byte)[:, None, :]).reshape(k, n).astype(np.float32)
    by_word = np.ascontiguousarray(scaled.reshape(k // 512, 128, 4, n).transpose(0, 1, 3, 2))
    if fmt == "e4m3":
        words = by_word.astype(ml_dtypes.float8_e4m3fn).view(np.uint8)
    else:
        c = by_word.astype(ml_dtypes.float4_e2m1fn).view(np.uint8) & 0xF
        words = (c[..., 0::2] | (c[..., 1::2] << 4)).reshape(k // 512, 128, 2 * n)
    return np.ascontiguousarray(words), np.ascontiguousarray(byte.astype(np.uint8).reshape(k // 512, 16, n))


def unpack_weight(words, scales, fmt):
    g, _, n = scales.shape
    words = np.ascontiguousarray(words).reshape(g, 128, n, -1)
    if fmt == "e4m3":
        vals = words.view(ml_dtypes.float8_e4m3fn).astype(np.float64)
    else:
        nib = np.empty((g, 128, n, 4), np.uint8)
        nib[..., 0::2] = words & 0xF
        nib[..., 1::2] = words >> 4
        vals = E2M1[nib]
    vals = vals * np.repeat(np.exp2(scales.astype(np.float64) - 127.0), 8, axis=1)[..., None]
    return vals.transpose(0, 1, 3, 2).reshape(g * 512, n)


def gelu(v):
    return 0.5 * v * (1.0 + np.tanh(np.sqrt(2.0 / np.pi) * (v + 0.044715 * v**3)))


def striped8(idx):
    return np.concatenate([v.reshape(-1, 16).T for v in idx]).astype(np.uint16)


def unstriped8(offs):
    return np.stack([offs[16 * g:16 * g + 16].T.reshape(-1) for g in range(8)]).astype(np.int64)


def runs(v, idx8):
    k = np.arange(v.shape[0])
    return v[k[:, None], idx8[k % 512 // 64]]


T, S, P, K, H, N = 2048, 1024, 512, 1024, 1024, 512

def setup_inputs():
    n = np.random.standard_normal
    s = mx_kscale(K)[:, None]
    u = mx_kscale(H)[:, None]
    d = {}
    d["tab_words"], d["tab_scales"] = pack_weight(n((K, T)) * s, "e4m3")
    d["offs"] = striped8(np.stack([np.random.permutation(T)[:S] for _ in range(8)]))
    d["pos1"] = striped(np.random.permutation(S)[:P])
    d["pos2"] = striped(np.random.permutation(S)[:P])
    d["w1"] = (n((K, H)) / s * u.T / K ** 0.5).astype(np.float32)
    d["w2_words"], d["w2_scales"] = pack_weight(n((K, H)) / s * u.T / K ** 0.5, "e2m1")
    d["b1"] = ((0.6 + 0.5 * n(H)) * u[:, 0]).astype(np.float32)
    d["gm"] = np.exp(0.5 * n((H, P))).astype(np.float32)
    d["w3"] = (1.5 * n((H, N)) / u / H ** 0.5).astype(np.float32)
    return d

def reference(tab_words, tab_scales, offs, pos1, pos2, w1, w2_words, w2_scales, b1, gm, w3):
    v = runs(unpack_weight(tab_words, tab_scales, "e4m3"), unstriped8(offs))
    w2 = unpack_weight(w2_words, w2_scales, "e2m1")
    y1 = mxq(f64(w1), 0, "e4m3").T @ v
    y2 = w2.T @ v
    h = np.minimum(y1, y2) + f64(b1)[:, None]
    before = h[:, unstriped(pos1)]
    after = h[:, unstriped(pos2)]
    z = np.maximum(before * f64(gm), after)
    y = mxq(f64(w3), 0, "e4m3").T @ mxq(z, 0, "e4m3")
    return np.log(1.0 + np.abs(y))

@@ -1,0 +1,330 @@
+from contextlib import ExitStack
+
+import concourse.mybir as mybir
+from concourse.masks import make_identity
+
+T, S, M, K, H, N = 2048, 1024, 512, 1024, 1024, 512
+FLOPS = 2 * 2 * K * H * S + 2 * H * N * M
+
+F32 = mybir.dt.float32
+BF16 = mybir.dt.bfloat16
+I32 = mybir.dt.int32
+U32 = mybir.dt.uint32
+U16 = mybir.dt.uint16
+U8 = mybir.dt.uint8
+FP8X4 = mybir.dt.float8_e4m3fn_x4
+FP4X4 = mybir.dt.float4_e2m1fn_x4
+ALU = mybir.AluOpType
+ACT = mybir.ActivationFunctionType
+
+P = 128
+PASS = 512
+BANK = 512
+PAIR_BYTES = 2 * 4 * PASS * 4
+CHUNKS = ((0, 256), (256, 384), (384, 512))
+
+
+def dealt_rows(x, b, t):
+    return x[PASS * b : PASS * (b + 1), :].rearrange("(j t e) n -> t j e n", t=4, e=8)[t]
+
+
+def tile_list_okta_cover_scores_kernel(
+    tc, tab_words, tab_scales, offs, pos1, pos2, w1, w2_words, w2_scales, b1, gm, w3, out
+):
+    nc = tc.nc
+    with ExitStack() as ctx:
+        keep = ctx.enter_context(tc.tile_pool(name="keep", bufs=1))
+        early = ctx.enter_context(tc.tile_pool(name="early", bufs=1))
+        ring = ctx.enter_context(tc.tile_pool(name="ring", bufs=2))
+        psum = ctx.enter_context(tc.psum_pool(name="psum", bufs=8))
+
+        offs_sb = keep.tile([P, S // 16], U16, name="offs_sb")
+        pos1_sb = keep.tile([P, M // 16], U16, name="pos1_sb")
+        pos2_sb = keep.tile([P, M // 16], U16, name="pos2_sb")
+        b_rows = keep.tile([P, P], F32, name="b_rows")
+        w2s_raw = keep.tile([P, 2, H], U8, name="w2s_raw", align_bytes=64)
+        v_scales = keep.tile([P, 2, S], U8, name="v_scales", align_bytes=64)
+        ident = keep.tile([P, P], F32, name="ident")
+
+        def wide_tile(slot, shape, dtype):
+            return keep.tile(shape, dtype, name=f"wide{slot}", tag=f"wide{slot}", align_bytes=64)
+
+        sc_win = early.tile([P, T], U8, name="sc_win", align_bytes=64, offset=PAIR_BYTES - T // 2)
+        nc.gpsimd.memset(sc_win[:].bitcast(I32), 0)
+        nc.gpsimd.memset(w2s_raw[:].rearrange("p a c -> p (a c)").bitcast(I32), 0)
+        nc.vector.memset(b_rows[:], 0.0)
+        nc.vector.memset(v_scales[:].rearrange("p a c -> p (a c)").bitcast(I32), 0)
+
+        nc.sync.dma_start(offs_sb[:], offs)
+        nc.scalar.dma_start(out=sc_win[0:P:4, :].bitcast(I32), in_=tab_scales.rearrange("a q t -> q a t").bitcast(I32))
+        tab_win = []
+        for a in range(2):
+            win = wide_tile(a, [P, T], U32)
+            nc.sync.dma_start(
+                out=win[:].bitcast(I32), in_=tab_words[a].rearrange("p t i -> p (t i)").bitcast(I32)
+            )
+            tab_win.append(win)
+
+        def load_w2(b):
+            raw = keep.tile([P, 2, 2 * PASS], U8, name="w2_raw", tag="w2_raw", align_bytes=64)
+            nc.sync.dma_start(
+                out=raw[:].bitcast(I32),
+                in_=w2_words[:, :, 2 * PASS * b : 2 * PASS * (b + 1)].rearrange("a p c -> p a c").bitcast(I32),
+            )
+            return raw
+
+        def load_w1(b, a, raw):
+            rows = w1[PASS * a : PASS * (a + 1), PASS * b : PASS * (b + 1)]
+            nc.sync.dma_start(out=raw, in_=rows.rearrange("(p i) c -> p i c", i=4))
+            return raw
+
+        def load_dealt(x, b, raw):
+            for t in range(4):
+                nc.sync.dma_start(out=raw[:, t, :], in_=dealt_rows(x, b, t))
+            return raw
+
+        def one_pass(slot):
+            return wide_tile(slot, [P, 4, PASS], F32)[:]
+
+        def two_passes():
+            both = early.tile([P, 2, 4, PASS], F32, name="both", tag="both", align_bytes=64, offset=0)
+            return both[:, 0], both[:, 1]
+
+        w2_raw = {0: load_w2(0)}
+        for d in range(4):
+            nc.scalar.dma_start(
+                out=w2s_raw[32 * d : 32 * d + 4].bitcast(I32),
+                in_=w2_scales[:, 4 * d : 4 * d + 4, :].rearrange("a r c -> r a c").bitcast(I32),
+            )
+        nc.sync.dma_start(pos1_sb[:], pos1)
+        nc.sync.dma_start(pos2_sb[:], pos2)
+
+        make_identity(nc, ident[:])
+        for b in range(2):
+            nc.gpsimd.dma_start(
+                out=b_rows[4 * b : 4 * b + 4, :].rearrange("t (j e) -> t j e", e=8),
+                in_=b1[PASS * b : PASS * (b + 1)].rearrange("(j t e) -> t j e", t=4, e=8),
+            )
+
+        sc_got = keep.tile([P, S], U8, name="sc_got", align_bytes=64)
+        nc.vector.tensor_copy(out=sc_got[:], in_=sc_win[:].indirect(offs_sb[:]))
+        for d in range(4):
+            nc.scalar.dma_start(
+                out=v_scales[32 * d : 32 * d + 4].bitcast(I32),
+                in_=sc_got[32 * d : 32 * d + 32 : 4, :].bitcast(I32),
+            )
+        w1_raw = {(0, a): load_w1(0, a, raw) for a, raw in enumerate(two_passes())}
+
+        v_codes = []
+        for a in range(2):
+            got = early.tile([P, S], U32, name=f"v_codes{a}", align_bytes=64, offset=PAIR_BYTES + 4 * S * a)
+            nc.vector.tensor_copy(out=got[:], in_=tab_win[a][:].indirect(offs_sb[:]))
+            v_codes.append(got)
+        gm_sb = {0: load_dealt(gm, 0, one_pass(0))}
+        w1_raw[1, 0] = load_w1(1, 0, one_pass(1))
+
+        b_bank = psum.tile([P, BANK], F32, name="bank", tag="bank")
+        nc.tensor.transpose(b_bank[:, 0:P], b_rows[:], ident[:])
+        b_cols = keep.tile([P, 8], F32, name="b_cols")
+        nc.scalar.copy(out=b_cols[:], in_=b_bank[:, 0:8])
+
+        w1_codes = [[keep.tile([P, 4, P], U32, name=f"w1_codes{b}{a}", align_bytes=64) for a in range(2)] for b in range(2)]
+        w1_scales = [[keep.tile([P, 4, P], U8, name=f"w1_scales{b}{a}", align_bytes=64) for a in range(2)] for b in range(2)]
+        w2_codes = [keep.tile([P, 2, 4, 2 * P], U8, name=f"w2_codes{b}", align_bytes=64) for b in range(2)]
+        w2_sc = [keep.tile([P, 2, 4, P], U8, name=f"w2_sc{b}", align_bytes=64) for b in range(2)]
+        w3_codes = [keep.tile([P, N], U32, name=f"w3_codes{b}", align_bytes=64) for b in range(2)]
+        w3_scales = [keep.tile([P, N], U8, name=f"w3_scales{b}", align_bytes=64) for b in range(2)]
+        z_codes = [keep.tile([P, M], U32, name=f"z_codes{b}", align_bytes=64) for b in range(2)]
+        z_scales = [keep.tile([P, M], U8, name=f"z_scales{b}", align_bytes=64) for b in range(2)]
+
+        def w1_staging():
+            return ring.tile([P, 4, 4 * P], BF16, name="bf", tag="bf", bufs=3, align_bytes=64)
+
+        def round_w1(copy, bf, b, a, t):
+            src = w1_raw[b, a].rearrange("p i (j t h l) -> p t j h i l", t=4, h=2, l=4)
+            copy(out=bf[:, t, :].rearrange("p (j h l i) -> p j h i l", h=2, l=4, i=4), in_=src[:, t])
+
+        def quantize_w1(bf, b, a, lo, hi):
+            nc.vector.quantize_mx(
+                out=w1_codes[b][a][:, lo:hi, :].rearrange("p t c -> p (t c)").bitcast(FP8X4),
+                scales=w1_scales[b][a][:, lo:hi, :].rearrange("p t c -> p (t c)"),
+                in_=bf[:, lo:hi, :].rearrange("p t c -> p (t c)"),
+            )
+
+        def deal_w2_scales(b):
+            nc.vector.tensor_copy(
+                out=w2_sc[b][:].bitcast(I32).rearrange("p a t (j w) -> p a t j w", w=2),
+                in_=w2s_raw[:, :, PASS * b : PASS * (b + 1)].bitcast(I32).rearrange("p a (j t w) -> p a t j w", t=4, w=2),
+            )
+
+        def deal_w2_codes(b):
+            nc.vector.tensor_copy(
+                out=w2_codes[b][:].bitcast(I32).rearrange("p a t (j w) -> p a t j w", w=4),
+                in_=w2_raw[b][:].bitcast(I32).rearrange("p a (j t w) -> p a t j w", t=4, w=4),
+            )
+
+        def round_w3(raw):
+            bf = ring.tile([P, 4 * N], BF16, name="bf", tag="bf", bufs=3, align_bytes=64)
+            for half in range(2):
+                cols = slice(half * (N // 2), (half + 1) * (N // 2))
+                nc.scalar.copy(
+                    out=bf[:, 2 * N * half : 2 * N * (half + 1)].rearrange("p (c l t) -> p c t l", l=4, t=4),
+                    in_=raw[:, :, cols].rearrange("p t (c l) -> p c t l", l=4),
+                )
+            return bf
+
+        def quantize_w3(bf, b):
+            nc.vector.quantize_mx(out=w3_codes[b][:].bitcast(FP8X4), scales=w3_scales[b][:], in_=bf[:])
+
+        def first_stage(b, t):
+            h = ring.tile([P, S], F32, name="h", tag="h", bufs=4, align_bytes=64)
+            bias = b_cols[:, 4 * b + t : 4 * b + t + 1]
+            for half in range(2):
+                cols = slice(half * BANK, (half + 1) * BANK)
+                y2 = psum.tile([P, BANK], F32, name="bank", tag="bank")
+                y1 = psum.tile([P, BANK], F32, name="bank", tag="bank")
+                for a in range(2):
+                    nc.tensor.matmul_mx(
+                        out=y2[:],
+                        lhsT=w2_codes[b][:, a, t, :].bitcast(FP4X4),
+                        lhsT_scale=w2_sc[b][:, a, t, :],
+                        rhs=v_codes[a][:, cols].bitcast(FP8X4),
+                        rhs_scale=v_scales[:, a, cols],
+                        start=(a == 0),
+                        stop=(a == 1),
+                    )
+                for a in range(2):
+                    nc.tensor.matmul_mx(
+                        out=y1[:],
+                        lhsT=w1_codes[b][a][:, t, :].bitcast(FP8X4),
+                        lhsT_scale=w1_scales[b][a][:, t, :],
+                        rhs=v_codes[a][:, cols].bitcast(FP8X4),
+                        rhs_scale=v_scales[:, a, cols],
+                        start=(a == 0),
+                        stop=(a == 1),
+                    )
+                y2b = ring.tile([P, BANK], F32, name="y2b", tag="y2b", bufs=4, align_bytes=64)
+                nc.scalar.activation(out=y2b[:], in_=y2[:], func=ACT.Identity, bias=bias)
+                nc.vector.scalar_tensor_tensor(
+                    out=h[:, cols], in0=y1[:], scalar=bias, in1=y2b[:], op0=ALU.add, op1=ALU.min
+                )
+            return h
+
+        before = keep.tile([P, 4, M], F32, name="before", align_bytes=64)
+        after = keep.tile([P, 4, M], F32, name="after", align_bytes=64)
+
+        def pick(h, b, t, lo, hi):
+            entries = slice(lo // 16, hi // 16)
+            nc.vector.tensor_copy(out=after[:, t, lo:hi], in_=h[:].indirect(pos2_sb[:, entries]))
+            nc.vector.tensor_tensor(
+                out=before[:, t, lo:hi], in0=h[:].indirect(pos1_sb[:, entries]), in1=gm_sb[b][:, t, lo:hi], op=ALU.mult
+            )
+
+        def meet(lo, hi):
+            z = ring.tile([P, 4 * (hi - lo)], BF16, name="z", tag="z", align_bytes=64)
+            nc.vector.tensor_tensor(
+                out=z[:].rearrange("p (c l t) -> p c t l", l=4, t=4),
+                in0=before[:, :, lo:hi].rearrange("p t (c l) -> p c t l", l=4),
+                in1=after[:, :, lo:hi].rearrange("p t (c l) -> p c t l", l=4),
+                op=ALU.max,
+            )
+            return z
+
+        def quantize_z(z, b, lo, hi):
+            nc.vector.quantize_mx(out=z_codes[b][:, lo:hi].bitcast(FP8X4), scales=z_scales[b][:, lo:hi], in_=z[:])
+
+        def second_stage_pass(banks, b, lo, hi):
+            width = hi - lo
+            for i in range(4):
+                n_cols = slice(i * P, (i + 1) * P)
+                nc.tensor.matmul_mx(
+                    out=banks[i // 2][:, (i % 2) * width : (i % 2 + 1) * width],
+                    lhsT=w3_codes[b][:, n_cols].bitcast(FP8X4),
+                    lhsT_scale=w3_scales[b][:, n_cols],
+                    rhs=z_codes[b][:, lo:hi].bitcast(FP8X4),
+                    rhs_scale=z_scales[b][:, lo:hi],
+                    start=(b == 0 and i % 2 == 0),
+                    stop=(b == 1 and i % 2 == 1),
+                )
+
+        def finish(banks, lo, hi):
+            width = hi - lo
+            sizes = []
+            for y in banks:
+                size = ring.tile([P, 2 * width], F32, name="size", tag="size", align_bytes=64)
+                nc.scalar.activation(out=size[:], in_=y[:, 0 : 2 * width], func=ACT.Abs)
+                sizes.append(size)
+            for pair, size in enumerate(sizes):
+                score = ring.tile([P, 2 * width], F32, name="score", tag="score", bufs=6, align_bytes=64)
+                nc.scalar.activation(out=score[:], in_=size[:], func=ACT.Ln, bias=1.0)
+                nc.sync.dma_start(
+                    out=out[2 * pair * P : 2 * (pair + 1) * P, lo:hi].rearrange("(i p) m -> p i m", p=P),
+                    in_=score[:].rearrange("p (i m) -> p i m", m=width),
+                )
+
+        on_scalar, on_vector = nc.scalar.copy, nc.vector.tensor_copy
+
+        deal_w2_scales(0)
+        deal_w2_codes(0)
+        deal_w2_scales(1)
+        w2_raw[1] = load_w2(1)
+        bf00 = w1_staging()
+        for t in range(4):
+            round_w1(on_scalar if t < 2 else on_vector, bf00, 0, 0, t)
+        quantize_w1(bf00, 0, 0, 0, 4)
+        bf01 = w1_staging()
+        round_w1(on_vector, bf01, 0, 1, 0)
+        quantize_w1(bf01, 0, 1, 0, 1)
+        h = {0: first_stage(0, 0)}
+        round_w1(on_scalar, bf01, 0, 1, 1)
+        quantize_w1(bf01, 0, 1, 1, 2)
+        h[1] = first_stage(0, 1)
+        round_w1(on_scalar, bf01, 0, 1, 2)
+        round_w1(on_scalar, bf01, 0, 1, 3)
+        quantize_w1(bf01, 0, 1, 2, 4)
+        w1_raw[1, 1], gm_sb[1] = two_passes()
+        load_w1(1, 1, w1_raw[1, 1])
+        load_dealt(gm, 1, gm_sb[1])
+        pick(h[0], 0, 0, 0, M)
+
+        h[2] = first_stage(0, 2)
+        bf10 = w1_staging()
+        for t in range(4):
+            round_w1(on_scalar, bf10, 1, 0, t)
+        w3_raw0 = load_dealt(w3, 0, one_pass(1))
+        pick(h[1], 0, 1, 0, M)
+        quantize_w1(bf10, 1, 0, 0, 4)
+        deal_w2_codes(1)
+
+        h[3] = first_stage(0, 3)
+        bf11 = w1_staging()
+        for t in range(4):
+            round_w1(on_scalar, bf11, 1, 1, t)
+        quantize_w1(bf11, 1, 1, 0, 4)
+        pick(h[2], 0, 2, 0, M)
+
+        h[4] = first_stage(1, 0)
+        pick(h[3], 0, 3, 0, M)
+        w3_raw1 = load_dealt(w3, 1, one_pass(0))
+        h[5] = first_stage(1, 1)
+        z = meet(0, M)
+        bf30 = round_w3(w3_raw0)
+        pick(h[4], 1, 0, 0, M)
+        quantize_z(z, 0, 0, M)
+        quantize_w3(bf30, 0)
+        h[6] = first_stage(1, 2)
+        bf31 = round_w3(w3_raw1)
+        h[7] = first_stage(1, 3)
+        quantize_w3(bf31, 1)
+
+        banks = {}
+        for lo, hi in CHUNKS:
+            banks[lo] = [psum.tile([P, BANK], F32, name="bank", tag="bank") for pair in range(2)]
+            second_stage_pass(banks[lo], 0, lo, hi)
+        for lo, hi in CHUNKS:
+            for t in range(1, 4):
+                pick(h[4 + t], 1, t, lo, hi)
+            z = meet(lo, hi)
+            quantize_z(z, 1, lo, hi)
+            second_stage_pass(banks[lo], 1, lo, hi)
+            finish(banks[lo], lo, hi)

@@ -20,8 +20,8 @@ ACT = mybir.ActivationFunctionType
 P = 128
 PASS = 512
 BANK = 512
-PAIR_BYTES = 2 * 4 * PASS * 4
-CHUNKS = ((0, 256), (256, 384), (384, 512))
+PASS_BYTES = 4 * PASS * 4
+CHUNK = 128
 
 
 def dealt_rows(x, b, t):
@@ -36,7 +36,7 @@ def tile_list_okta_cover_scores_kernel(
         keep = ctx.enter_context(tc.tile_pool(name="keep", bufs=1))
         early = ctx.enter_context(tc.tile_pool(name="early", bufs=1))
         ring = ctx.enter_context(tc.tile_pool(name="ring", bufs=2))
-        psum = ctx.enter_context(tc.psum_pool(name="psum", bufs=8))
+        psum = ctx.enter_context(tc.psum_pool(name="psum", bufs=1))
 
         offs_sb = keep.tile([P, S // 16], U16, name="offs_sb")
         pos1_sb = keep.tile([P, M // 16], U16, name="pos1_sb")
@@ -49,21 +49,19 @@ def tile_list_okta_cover_scores_kernel(
         def wide_tile(slot, shape, dtype):
             return keep.tile(shape, dtype, name=f"wide{slot}", tag=f"wide{slot}", align_bytes=64)
 
-        sc_win = early.tile([P, T], U8, name="sc_win", align_bytes=64, offset=PAIR_BYTES - T // 2)
-        nc.gpsimd.memset(sc_win[:].bitcast(I32), 0)
-        nc.gpsimd.memset(w2s_raw[:].rearrange("p a c -> p (a c)").bitcast(I32), 0)
-        nc.vector.memset(b_rows[:], 0.0)
+        sc_win = early.tile([P, T], U8, name="sc_win", align_bytes=64, offset=PASS_BYTES - T // 2)
+        nc.gpsimd.memset(b_rows[:], 0.0)
+        nc.vector.memset(w2s_raw[:].rearrange("p a c -> p (a c)").bitcast(I32), 0)
         nc.vector.memset(v_scales[:].rearrange("p a c -> p (a c)").bitcast(I32), 0)
 
         nc.sync.dma_start(offs_sb[:], offs)
-        nc.scalar.dma_start(out=sc_win[0:P:4, :].bitcast(I32), in_=tab_scales.rearrange("a q t -> q a t").bitcast(I32))
-        tab_win = []
-        for a in range(2):
-            win = wide_tile(a, [P, T], U32)
-            nc.sync.dma_start(
-                out=win[:].bitcast(I32), in_=tab_words[a].rearrange("p t i -> p (t i)").bitcast(I32)
+        for b in range(2):
+            nc.gpsimd.dma_start(
+                out=b_rows[4 * b : 4 * b + 4, :].rearrange("t (j e) -> t j e", e=8),
+                in_=b1[PASS * b : PASS * (b + 1)].rearrange("(j t e) -> t j e", t=4, e=8),
             )
-            tab_win.append(win)
+        for x in range(4):
+            nc.sync.dma_start(out=sc_win[x:P:4, :].bitcast(I32), in_=tab_scales.rearrange("a q t -> q a t").bitcast(I32))
 
         def load_w2(b):
             raw = keep.tile([P, 2, 2 * PASS], U8, name="w2_raw", tag="w2_raw", align_bytes=64)
@@ -86,59 +84,63 @@ def tile_list_okta_cover_scores_kernel(
         def one_pass(slot):
             return wide_tile(slot, [P, 4, PASS], F32)[:]
 
-        def two_passes():
-            both = early.tile([P, 2, 4, PASS], F32, name="both", tag="both", align_bytes=64, offset=0)
-            return both[:, 0], both[:, 1]
+        def early_pass(slot):
+            name = f"early{slot}"
+            return early.tile([P, 4, PASS], F32, name=name, tag=name, align_bytes=64, offset=slot * PASS_BYTES)[:]
 
         w2_raw = {0: load_w2(0)}
+        tab_win = []
+        for a in range(2):
+            win = wide_tile(a, [P, T], U32)
+            nc.sync.dma_start(
+                out=win[:].bitcast(I32), in_=tab_words[a].rearrange("p t i -> p (t i)").bitcast(I32)
+            )
+            tab_win.append(win)
+        nc.sync.dma_start(pos1_sb[:], pos1)
+        nc.sync.dma_start(pos2_sb[:], pos2)
         for d in range(4):
             nc.scalar.dma_start(
                 out=w2s_raw[32 * d : 32 * d + 4].bitcast(I32),
                 in_=w2_scales[:, 4 * d : 4 * d + 4, :].rearrange("a r c -> r a c").bitcast(I32),
             )
-        nc.sync.dma_start(pos1_sb[:], pos1)
-        nc.sync.dma_start(pos2_sb[:], pos2)
-
         make_identity(nc, ident[:])
-        for b in range(2):
-            nc.gpsimd.dma_start(
-                out=b_rows[4 * b : 4 * b + 4, :].rearrange("t (j e) -> t j e", e=8),
-                in_=b1[PASS * b : PASS * (b + 1)].rearrange("(j t e) -> t j e", t=4, e=8),
-            )
 
         sc_got = keep.tile([P, S], U8, name="sc_got", align_bytes=64)
         nc.vector.tensor_copy(out=sc_got[:], in_=sc_win[:].indirect(offs_sb[:]))
         for d in range(4):
-            nc.scalar.dma_start(
+            nc.sync.dma_start(
                 out=v_scales[32 * d : 32 * d + 4].bitcast(I32),
                 in_=sc_got[32 * d : 32 * d + 32 : 4, :].bitcast(I32),
             )
-        w1_raw = {(0, a): load_w1(0, a, raw) for a, raw in enumerate(two_passes())}
+        w1_raw = {(0, a): load_w1(0, a, early_pass(a)) for a in range(2)}
 
         v_codes = []
         for a in range(2):
-            got = early.tile([P, S], U32, name=f"v_codes{a}", align_bytes=64, offset=PAIR_BYTES + 4 * S * a)
+            got = keep.tile([P, S], U32, name=f"v_codes{a}", align_bytes=64)
             nc.vector.tensor_copy(out=got[:], in_=tab_win[a][:].indirect(offs_sb[:]))
             v_codes.append(got)
         gm_sb = {0: load_dealt(gm, 0, one_pass(0))}
         w1_raw[1, 0] = load_w1(1, 0, one_pass(1))
 
-        b_bank = psum.tile([P, BANK], F32, name="bank", tag="bank")
+        b_bank = psum.tile([P, BANK], F32, name="b_bank", tag="y1", bufs=6)
         nc.tensor.transpose(b_bank[:, 0:P], b_rows[:], ident[:])
         b_cols = keep.tile([P, 8], F32, name="b_cols")
         nc.scalar.copy(out=b_cols[:], in_=b_bank[:, 0:8])
 
         w1_codes = [[keep.tile([P, 4, P], U32, name=f"w1_codes{b}{a}", align_bytes=64) for a in range(2)] for b in range(2)]
         w1_scales = [[keep.tile([P, 4, P], U8, name=f"w1_scales{b}{a}", align_bytes=64) for a in range(2)] for b in range(2)]
-        w2_codes = [keep.tile([P, 2, 4, 2 * P], U8, name=f"w2_codes{b}", align_bytes=64) for b in range(2)]
+        w2_codes = {}
         w2_sc = [keep.tile([P, 2, 4, P], U8, name=f"w2_sc{b}", align_bytes=64) for b in range(2)]
         w3_codes = [keep.tile([P, N], U32, name=f"w3_codes{b}", align_bytes=64) for b in range(2)]
         w3_scales = [keep.tile([P, N], U8, name=f"w3_scales{b}", align_bytes=64) for b in range(2)]
         z_codes = [keep.tile([P, M], U32, name=f"z_codes{b}", align_bytes=64) for b in range(2)]
         z_scales = [keep.tile([P, M], U8, name=f"z_scales{b}", align_bytes=64) for b in range(2)]
 
-        def w1_staging():
-            return ring.tile([P, 4, 4 * P], BF16, name="bf", tag="bf", bufs=3, align_bytes=64)
+        def chain_tile(chain, shape, dtype):
+            return keep.tile(shape, dtype, name=f"chain{chain}", tag=f"chain{chain}", align_bytes=64)
+
+        def w1_staging(chain):
+            return chain_tile(chain, [P, 4, 4 * P], BF16)
 
         def round_w1(copy, bf, b, a, t):
             src = w1_raw[b, a].rearrange("p i (j t h l) -> p t j h i l", t=4, h=2, l=4)
@@ -158,13 +160,14 @@ def tile_list_okta_cover_scores_kernel(
             )
 
         def deal_w2_codes(b):
+            w2_codes[b] = chain_tile(8 + b, [P, 2, 4, 2 * P], U8)
             nc.vector.tensor_copy(
                 out=w2_codes[b][:].bitcast(I32).rearrange("p a t (j w) -> p a t j w", w=4),
                 in_=w2_raw[b][:].bitcast(I32).rearrange("p a (j t w) -> p a t j w", t=4, w=4),
             )
 
-        def round_w3(raw):
-            bf = ring.tile([P, 4 * N], BF16, name="bf", tag="bf", bufs=3, align_bytes=64)
+        def round_w3(raw, chain):
+            bf = chain_tile(chain, [P, 4 * N], BF16)
             for half in range(2):
                 cols = slice(half * (N // 2), (half + 1) * (N // 2))
                 nc.scalar.copy(
@@ -177,12 +180,12 @@ def tile_list_okta_cover_scores_kernel(
             nc.vector.quantize_mx(out=w3_codes[b][:].bitcast(FP8X4), scales=w3_scales[b][:], in_=bf[:])
 
         def first_stage(b, t):
-            h = ring.tile([P, S], F32, name="h", tag="h", bufs=4, align_bytes=64)
+            h = chain_tile(4 * b + t, [P, S], F32)
             bias = b_cols[:, 4 * b + t : 4 * b + t + 1]
             for half in range(2):
                 cols = slice(half * BANK, (half + 1) * BANK)
-                y2 = psum.tile([P, BANK], F32, name="bank", tag="bank")
-                y1 = psum.tile([P, BANK], F32, name="bank", tag="bank")
+                y2 = psum.tile([P, BANK], F32, name="y2", tag="y2", bufs=2)
+                y1 = psum.tile([P, BANK], F32, name="y1", tag="y1", bufs=6)
                 for a in range(2):
                     nc.tensor.matmul_mx(
                         out=y2[:],
@@ -203,29 +206,38 @@ def tile_list_okta_cover_scores_kernel(
                         start=(a == 0),
                         stop=(a == 1),
                     )
-                y2b = ring.tile([P, BANK], F32, name="y2b", tag="y2b", bufs=4, align_bytes=64)
+                if (b, t) == (0, 2):
+                    y2b = chain_tile(9 + half, [P, BANK], F32)
+                elif (b, t) == (0, 0):
+                    y2b = early.tile([P, BANK], F32, name=f"y2b_first{half}", align_bytes=64, offset=half * 4 * BANK)
+                else:
+                    y2b = ring.tile([P, BANK], F32, name="y2b", tag="y2b", bufs=4, align_bytes=64)
                 nc.scalar.activation(out=y2b[:], in_=y2[:], func=ACT.Identity, bias=bias)
                 nc.vector.scalar_tensor_tensor(
                     out=h[:, cols], in0=y1[:], scalar=bias, in1=y2b[:], op0=ALU.add, op1=ALU.min
                 )
             return h
 
-        before = keep.tile([P, 4, M], F32, name="before", align_bytes=64)
-        after = keep.tile([P, 4, M], F32, name="after", align_bytes=64)
+        def picked_pair(width):
+            before = ring.tile([P, 4, width], F32, name="before", tag=f"before{width}", align_bytes=64)
+            after = ring.tile([P, 4, width], F32, name="after", tag=f"after{width}", align_bytes=64)
+            return before, after
 
-        def pick(h, b, t, lo, hi):
+        def pick(pair, h, b, t, lo, hi):
+            before, after = pair
             entries = slice(lo // 16, hi // 16)
-            nc.vector.tensor_copy(out=after[:, t, lo:hi], in_=h[:].indirect(pos2_sb[:, entries]))
+            nc.vector.tensor_copy(out=after[:, t, :], in_=h[:].indirect(pos2_sb[:, entries]))
             nc.vector.tensor_tensor(
-                out=before[:, t, lo:hi], in0=h[:].indirect(pos1_sb[:, entries]), in1=gm_sb[b][:, t, lo:hi], op=ALU.mult
+                out=before[:, t, :], in0=h[:].indirect(pos1_sb[:, entries]), in1=gm_sb[b][:, t, lo:hi], op=ALU.mult
             )
 
-        def meet(lo, hi):
-            z = ring.tile([P, 4 * (hi - lo)], BF16, name="z", tag="z", align_bytes=64)
+        def meet(pair, width):
+            before, after = pair
+            z = ring.tile([P, 4 * width], BF16, name="z", tag="z", align_bytes=64)
             nc.vector.tensor_tensor(
                 out=z[:].rearrange("p (c l t) -> p c t l", l=4, t=4),
-                in0=before[:, :, lo:hi].rearrange("p t (c l) -> p c t l", l=4),
-                in1=after[:, :, lo:hi].rearrange("p t (c l) -> p c t l", l=4),
+                in0=before[:].rearrange("p t (c l) -> p c t l", l=4),
+                in1=after[:].rearrange("p t (c l) -> p c t l", l=4),
                 op=ALU.max,
             )
             return z
@@ -255,7 +267,7 @@ def tile_list_okta_cover_scores_kernel(
                 nc.scalar.activation(out=size[:], in_=y[:, 0 : 2 * width], func=ACT.Abs)
                 sizes.append(size)
             for pair, size in enumerate(sizes):
-                score = ring.tile([P, 2 * width], F32, name="score", tag="score", bufs=6, align_bytes=64)
+                score = ring.tile([P, 2 * width], F32, name="score", tag="score", bufs=8, align_bytes=64)
                 nc.scalar.activation(out=score[:], in_=size[:], func=ACT.Ln, bias=1.0)
                 nc.sync.dma_start(
                     out=out[2 * pair * P : 2 * (pair + 1) * P, lo:hi].rearrange("(i p) m -> p i m", p=P),
@@ -268,63 +280,63 @@ def tile_list_okta_cover_scores_kernel(
         deal_w2_codes(0)
         deal_w2_scales(1)
         w2_raw[1] = load_w2(1)
-        bf00 = w1_staging()
-        for t in range(4):
-            round_w1(on_scalar if t < 2 else on_vector, bf00, 0, 0, t)
-        quantize_w1(bf00, 0, 0, 0, 4)
-        bf01 = w1_staging()
+        bf00 = w1_staging(1)
+        round_w1(on_scalar, bf00, 0, 0, 0)
+        quantize_w1(bf00, 0, 0, 0, 1)
+        for t in range(1, 4):
+            round_w1(on_scalar, bf00, 0, 0, t)
+        bf01 = w1_staging(2)
         round_w1(on_vector, bf01, 0, 1, 0)
         quantize_w1(bf01, 0, 1, 0, 1)
         h = {0: first_stage(0, 0)}
+        quantize_w1(bf00, 0, 0, 1, 4)
         round_w1(on_scalar, bf01, 0, 1, 1)
         quantize_w1(bf01, 0, 1, 1, 2)
-        h[1] = first_stage(0, 1)
+        w1_raw[1, 1] = load_w1(1, 1, early_pass(0))
         round_w1(on_scalar, bf01, 0, 1, 2)
         round_w1(on_scalar, bf01, 0, 1, 3)
+        gm_sb[1] = load_dealt(gm, 1, early_pass(1))
+        pair = picked_pair(M)
+        pick(pair, h[0], 0, 0, 0, M)
         quantize_w1(bf01, 0, 1, 2, 4)
-        w1_raw[1, 1], gm_sb[1] = two_passes()
-        load_w1(1, 1, w1_raw[1, 1])
-        load_dealt(gm, 1, gm_sb[1])
-        pick(h[0], 0, 0, 0, M)
-
-        h[2] = first_stage(0, 2)
-        bf10 = w1_staging()
+        h[1] = first_stage(0, 1)
+        bf10 = w1_staging(0)
         for t in range(4):
             round_w1(on_scalar, bf10, 1, 0, t)
         w3_raw0 = load_dealt(w3, 0, one_pass(1))
-        pick(h[1], 0, 1, 0, M)
-        quantize_w1(bf10, 1, 0, 0, 4)
-        deal_w2_codes(1)
-
-        h[3] = first_stage(0, 3)
-        bf11 = w1_staging()
+        h[2] = first_stage(0, 2)
+        bf11 = w1_staging(10)
         for t in range(4):
             round_w1(on_scalar, bf11, 1, 1, t)
+        pick(pair, h[1], 0, 1, 0, M)
+        quantize_w1(bf10, 1, 0, 0, 4)
+        h[3] = first_stage(0, 3)
+        deal_w2_codes(1)
         quantize_w1(bf11, 1, 1, 0, 4)
-        pick(h[2], 0, 2, 0, M)
-
+        bf30 = round_w3(w3_raw0, 1)
+        w3_raw1 = load_dealt(w3, 1, one_pass(1))
+        pick(pair, h[2], 0, 2, 0, M)
         h[4] = first_stage(1, 0)
-        pick(h[3], 0, 3, 0, M)
-        w3_raw1 = load_dealt(w3, 1, one_pass(0))
+        bf31 = round_w3(w3_raw1, 2)
+        pick(pair, h[3], 0, 3, 0, M)
         h[5] = first_stage(1, 1)
-        z = meet(0, M)
-        bf30 = round_w3(w3_raw0)
-        pick(h[4], 1, 0, 0, M)
+        z = meet(pair, M)
+        h[6] = first_stage(1, 2)
         quantize_z(z, 0, 0, M)
         quantize_w3(bf30, 0)
-        h[6] = first_stage(1, 2)
-        bf31 = round_w3(w3_raw1)
         h[7] = first_stage(1, 3)
         quantize_w3(bf31, 1)
 
         banks = {}
-        for lo, hi in CHUNKS:
-            banks[lo] = [psum.tile([P, BANK], F32, name="bank", tag="bank") for pair in range(2)]
-            second_stage_pass(banks[lo], 0, lo, hi)
-        for lo, hi in CHUNKS:
-            for t in range(1, 4):
-                pick(h[4 + t], 1, t, lo, hi)
-            z = meet(lo, hi)
-            quantize_z(z, 1, lo, hi)
-            second_stage_pass(banks[lo], 1, lo, hi)
-            finish(banks[lo], lo, hi)
+        for lo in range(0, M, CHUNK):
+            tag, bufs = ("y2", 2) if lo == 0 else ("y1", 6)
+            banks[lo] = [psum.tile([P, BANK], F32, name="y", tag=tag, bufs=bufs) for i in range(2)]
+            second_stage_pass(banks[lo], 0, lo, lo + CHUNK)
+        for lo in range(0, M, CHUNK):
+            pair = picked_pair(CHUNK)
+            for t in range(4):
+                pick(pair, h[4 + t], 1, t, lo, lo + CHUNK)
+            z = meet(pair, CHUNK)
+            quantize_z(z, 1, lo, lo + CHUNK)
+            second_stage_pass(banks[lo], 1, lo, lo + CHUNK)
+            finish(banks[lo], lo, lo + CHUNK)

from contextlib import ExitStack

import concourse.mybir as mybir
from concourse.masks import make_identity

T, S, M, K, H, N = 2048, 1024, 512, 1024, 1024, 512
FLOPS = 2 * 2 * K * H * S + 2 * H * N * M

F32 = mybir.dt.float32
BF16 = mybir.dt.bfloat16
I32 = mybir.dt.int32
U32 = mybir.dt.uint32
U16 = mybir.dt.uint16
U8 = mybir.dt.uint8
FP8X4 = mybir.dt.float8_e4m3fn_x4
FP4X4 = mybir.dt.float4_e2m1fn_x4
ALU = mybir.AluOpType
ACT = mybir.ActivationFunctionType

P = 128
PASS = 512
BANK = 512
PASS_BYTES = 4 * PASS * 4
CHUNK = 128


def dealt_rows(x, b, t):
    return x[PASS * b : PASS * (b + 1), :].rearrange("(j t e) n -> t j e n", t=4, e=8)[t]


def tile_list_okta_cover_scores_kernel(
    tc, tab_words, tab_scales, offs, pos1, pos2, w1, w2_words, w2_scales, b1, gm, w3, out
):
    nc = tc.nc
    with ExitStack() as ctx:
        keep = ctx.enter_context(tc.tile_pool(name="keep", bufs=1))
        early = ctx.enter_context(tc.tile_pool(name="early", bufs=1))
        ring = ctx.enter_context(tc.tile_pool(name="ring", bufs=2))
        psum = ctx.enter_context(tc.psum_pool(name="psum", bufs=1))

        offs_sb = keep.tile([P, S // 16], U16, name="offs_sb")
        pos1_sb = keep.tile([P, M // 16], U16, name="pos1_sb")
        pos2_sb = keep.tile([P, M // 16], U16, name="pos2_sb")
        b_rows = keep.tile([P, P], F32, name="b_rows")
        w2s_raw = keep.tile([P, 2, H], U8, name="w2s_raw", align_bytes=64)
        v_scales = keep.tile([P, 2, S], U8, name="v_scales", align_bytes=64)
        ident = keep.tile([P, P], F32, name="ident")

        def wide_tile(slot, shape, dtype):
            return keep.tile(shape, dtype, name=f"wide{slot}", tag=f"wide{slot}", align_bytes=64)

        sc_win = early.tile([P, T], U8, name="sc_win", align_bytes=64, offset=PASS_BYTES - T // 2)
        nc.gpsimd.memset(b_rows[:], 0.0)
        nc.vector.memset(w2s_raw[:].rearrange("p a c -> p (a c)").bitcast(I32), 0)
        nc.vector.memset(v_scales[:].rearrange("p a c -> p (a c)").bitcast(I32), 0)

        nc.sync.dma_start(offs_sb[:], offs)
        for b in range(2):
            nc.gpsimd.dma_start(
                out=b_rows[4 * b : 4 * b + 4, :].rearrange("t (j e) -> t j e", e=8),
                in_=b1[PASS * b : PASS * (b + 1)].rearrange("(j t e) -> t j e", t=4, e=8),
            )
        for x in range(4):
            nc.sync.dma_start(out=sc_win[x:P:4, :].bitcast(I32), in_=tab_scales.rearrange("a q t -> q a t").bitcast(I32))

        def load_w2(b):
            raw = keep.tile([P, 2, 2 * PASS], U8, name="w2_raw", tag="w2_raw", align_bytes=64)
            nc.sync.dma_start(
                out=raw[:].bitcast(I32),
                in_=w2_words[:, :, 2 * PASS * b : 2 * PASS * (b + 1)].rearrange("a p c -> p a c").bitcast(I32),
            )
            return raw

        def load_w1(b, a, raw):
            rows = w1[PASS * a : PASS * (a + 1), PASS * b : PASS * (b + 1)]
            nc.sync.dma_start(out=raw, in_=rows.rearrange("(p i) c -> p i c", i=4))
            return raw

        def load_dealt(x, b, raw):
            for t in range(4):
                nc.sync.dma_start(out=raw[:, t, :], in_=dealt_rows(x, b, t))
            return raw

        def one_pass(slot):
            return wide_tile(slot, [P, 4, PASS], F32)[:]

        def early_pass(slot):
            name = f"early{slot}"
            return early.tile([P, 4, PASS], F32, name=name, tag=name, align_bytes=64, offset=slot * PASS_BYTES)[:]

        w2_raw = {0: load_w2(0)}
        tab_win = []
        for a in range(2):
            win = wide_tile(a, [P, T], U32)
            nc.sync.dma_start(
                out=win[:].bitcast(I32), in_=tab_words[a].rearrange("p t i -> p (t i)").bitcast(I32)
            )
            tab_win.append(win)
        nc.sync.dma_start(pos1_sb[:], pos1)
        nc.sync.dma_start(pos2_sb[:], pos2)
        for d in range(4):
            nc.scalar.dma_start(
                out=w2s_raw[32 * d : 32 * d + 4].bitcast(I32),
                in_=w2_scales[:, 4 * d : 4 * d + 4, :].rearrange("a r c -> r a c").bitcast(I32),
            )
        make_identity(nc, ident[:])

        sc_got = keep.tile([P, S], U8, name="sc_got", align_bytes=64)
        nc.vector.tensor_copy(out=sc_got[:], in_=sc_win[:].indirect(offs_sb[:]))
        for d in range(4):
            nc.sync.dma_start(
                out=v_scales[32 * d : 32 * d + 4].bitcast(I32),
                in_=sc_got[32 * d : 32 * d + 32 : 4, :].bitcast(I32),
            )
        w1_raw = {(0, a): load_w1(0, a, early_pass(a)) for a in range(2)}

        v_codes = []
        for a in range(2):
            got = keep.tile([P, S], U32, name=f"v_codes{a}", align_bytes=64)
            nc.vector.tensor_copy(out=got[:], in_=tab_win[a][:].indirect(offs_sb[:]))
            v_codes.append(got)
        gm_sb = {0: load_dealt(gm, 0, one_pass(0))}
        w1_raw[1, 0] = load_w1(1, 0, one_pass(1))

        b_bank = psum.tile([P, BANK], F32, name="b_bank", tag="y1", bufs=6)
        nc.tensor.transpose(b_bank[:, 0:P], b_rows[:], ident[:])
        b_cols = keep.tile([P, 8], F32, name="b_cols")
        nc.scalar.copy(out=b_cols[:], in_=b_bank[:, 0:8])

        w1_codes = [[keep.tile([P, 4, P], U32, name=f"w1_codes{b}{a}", align_bytes=64) for a in range(2)] for b in range(2)]
        w1_scales = [[keep.tile([P, 4, P], U8, name=f"w1_scales{b}{a}", align_bytes=64) for a in range(2)] for b in range(2)]
        w2_codes = {}
        w2_sc = [keep.tile([P, 2, 4, P], U8, name=f"w2_sc{b}", align_bytes=64) for b in range(2)]
        w3_codes = [keep.tile([P, N], U32, name=f"w3_codes{b}", align_bytes=64) for b in range(2)]
        w3_scales = [keep.tile([P, N], U8, name=f"w3_scales{b}", align_bytes=64) for b in range(2)]
        z_codes = [keep.tile([P, M], U32, name=f"z_codes{b}", align_bytes=64) for b in range(2)]
        z_scales = [keep.tile([P, M], U8, name=f"z_scales{b}", align_bytes=64) for b in range(2)]

        def chain_tile(chain, shape, dtype):
            return keep.tile(shape, dtype, name=f"chain{chain}", tag=f"chain{chain}", align_bytes=64)

        def w1_staging(chain):
            return chain_tile(chain, [P, 4, 4 * P], BF16)

        def round_w1(copy, bf, b, a, t):
            src = w1_raw[b, a].rearrange("p i (j t h l) -> p t j h i l", t=4, h=2, l=4)
            copy(out=bf[:, t, :].rearrange("p (j h l i) -> p j h i l", h=2, l=4, i=4), in_=src[:, t])

        def quantize_w1(bf, b, a, lo, hi):
            nc.vector.quantize_mx(
                out=w1_codes[b][a][:, lo:hi, :].rearrange("p t c -> p (t c)").bitcast(FP8X4),
                scales=w1_scales[b][a][:, lo:hi, :].rearrange("p t c -> p (t c)"),
                in_=bf[:, lo:hi, :].rearrange("p t c -> p (t c)"),
            )

        def deal_w2_scales(b):
            nc.vector.tensor_copy(
                out=w2_sc[b][:].bitcast(I32).rearrange("p a t (j w) -> p a t j w", w=2),
                in_=w2s_raw[:, :, PASS * b : PASS * (b + 1)].bitcast(I32).rearrange("p a (j t w) -> p a t j w", t=4, w=2),
            )

        def deal_w2_codes(b):
            w2_codes[b] = chain_tile(8 + b, [P, 2, 4, 2 * P], U8)
            nc.vector.tensor_copy(
                out=w2_codes[b][:].bitcast(I32).rearrange("p a t (j w) -> p a t j w", w=4),
                in_=w2_raw[b][:].bitcast(I32).rearrange("p a (j t w) -> p a t j w", t=4, w=4),
            )

        def round_w3(raw, chain):
            bf = chain_tile(chain, [P, 4 * N], BF16)
            for half in range(2):
                cols = slice(half * (N // 2), (half + 1) * (N // 2))
                nc.scalar.copy(
                    out=bf[:, 2 * N * half : 2 * N * (half + 1)].rearrange("p (c l t) -> p c t l", l=4, t=4),
                    in_=raw[:, :, cols].rearrange("p t (c l) -> p c t l", l=4),
                )
            return bf

        def quantize_w3(bf, b):
            nc.vector.quantize_mx(out=w3_codes[b][:].bitcast(FP8X4), scales=w3_scales[b][:], in_=bf[:])

        def first_stage(b, t):
            h = chain_tile(4 * b + t, [P, S], F32)
            bias = b_cols[:, 4 * b + t : 4 * b + t + 1]
            for half in range(2):
                cols = slice(half * BANK, (half + 1) * BANK)
                y2 = psum.tile([P, BANK], F32, name="y2", tag="y2", bufs=2)
                y1 = psum.tile([P, BANK], F32, name="y1", tag="y1", bufs=6)
                for a in range(2):
                    nc.tensor.matmul_mx(
                        out=y2[:],
                        lhsT=w2_codes[b][:, a, t, :].bitcast(FP4X4),
                        lhsT_scale=w2_sc[b][:, a, t, :],
                        rhs=v_codes[a][:, cols].bitcast(FP8X4),
                        rhs_scale=v_scales[:, a, cols],
                        start=(a == 0),
                        stop=(a == 1),
                    )
                for a in range(2):
                    nc.tensor.matmul_mx(
                        out=y1[:],
                        lhsT=w1_codes[b][a][:, t, :].bitcast(FP8X4),
                        lhsT_scale=w1_scales[b][a][:, t, :],
                        rhs=v_codes[a][:, cols].bitcast(FP8X4),
                        rhs_scale=v_scales[:, a, cols],
                        start=(a == 0),
                        stop=(a == 1),
                    )
                if (b, t) == (0, 2):
                    y2b = chain_tile(9 + half, [P, BANK], F32)
                elif (b, t) == (0, 0):
                    y2b = early.tile([P, BANK], F32, name=f"y2b_first{half}", align_bytes=64, offset=half * 4 * BANK)
                else:
                    y2b = ring.tile([P, BANK], F32, name="y2b", tag="y2b", bufs=4, align_bytes=64)
                nc.scalar.activation(out=y2b[:], in_=y2[:], func=ACT.Identity, bias=bias)
                nc.vector.scalar_tensor_tensor(
                    out=h[:, cols], in0=y1[:], scalar=bias, in1=y2b[:], op0=ALU.add, op1=ALU.min
                )
            return h

        def picked_pair(width):
            before = ring.tile([P, 4, width], F32, name="before", tag=f"before{width}", align_bytes=64)
            after = ring.tile([P, 4, width], F32, name="after", tag=f"after{width}", align_bytes=64)
            return before, after

        def pick(pair, h, b, t, lo, hi):
            before, after = pair
            entries = slice(lo // 16, hi // 16)
            nc.vector.tensor_copy(out=after[:, t, :], in_=h[:].indirect(pos2_sb[:, entries]))
            nc.vector.tensor_tensor(
                out=before[:, t, :], in0=h[:].indirect(pos1_sb[:, entries]), in1=gm_sb[b][:, t, lo:hi], op=ALU.mult
            )

        def meet(pair, width):
            before, after = pair
            z = ring.tile([P, 4 * width], BF16, name="z", tag="z", align_bytes=64)
            nc.vector.tensor_tensor(
                out=z[:].rearrange("p (c l t) -> p c t l", l=4, t=4),
                in0=before[:].rearrange("p t (c l) -> p c t l", l=4),
                in1=after[:].rearrange("p t (c l) -> p c t l", l=4),
                op=ALU.max,
            )
            return z

        def quantize_z(z, b, lo, hi):
            nc.vector.quantize_mx(out=z_codes[b][:, lo:hi].bitcast(FP8X4), scales=z_scales[b][:, lo:hi], in_=z[:])

        def second_stage_pass(banks, b, lo, hi):
            width = hi - lo
            for i in range(4):
                n_cols = slice(i * P, (i + 1) * P)
                nc.tensor.matmul_mx(
                    out=banks[i // 2][:, (i % 2) * width : (i % 2 + 1) * width],
                    lhsT=w3_codes[b][:, n_cols].bitcast(FP8X4),
                    lhsT_scale=w3_scales[b][:, n_cols],
                    rhs=z_codes[b][:, lo:hi].bitcast(FP8X4),
                    rhs_scale=z_scales[b][:, lo:hi],
                    start=(b == 0 and i % 2 == 0),
                    stop=(b == 1 and i % 2 == 1),
                )

        def finish(banks, lo, hi):
            width = hi - lo
            sizes = []
            for y in banks:
                size = ring.tile([P, 2 * width], F32, name="size", tag="size", align_bytes=64)
                nc.scalar.activation(out=size[:], in_=y[:, 0 : 2 * width], func=ACT.Abs)
                sizes.append(size)
            for pair, size in enumerate(sizes):
                score = ring.tile([P, 2 * width], F32, name="score", tag="score", bufs=8, align_bytes=64)
                nc.scalar.activation(out=score[:], in_=size[:], func=ACT.Ln, bias=1.0)
                nc.sync.dma_start(
                    out=out[2 * pair * P : 2 * (pair + 1) * P, lo:hi].rearrange("(i p) m -> p i m", p=P),
                    in_=score[:].rearrange("p (i m) -> p i m", m=width),
                )

        on_scalar, on_vector = nc.scalar.copy, nc.vector.tensor_copy

        deal_w2_scales(0)
        deal_w2_codes(0)
        deal_w2_scales(1)
        w2_raw[1] = load_w2(1)
        bf00 = w1_staging(1)
        round_w1(on_scalar, bf00, 0, 0, 0)
        quantize_w1(bf00, 0, 0, 0, 1)
        for t in range(1, 4):
            round_w1(on_scalar, bf00, 0, 0, t)
        bf01 = w1_staging(2)
        round_w1(on_vector, bf01, 0, 1, 0)
        quantize_w1(bf01, 0, 1, 0, 1)
        h = {0: first_stage(0, 0)}
        quantize_w1(bf00, 0, 0, 1, 4)
        round_w1(on_scalar, bf01, 0, 1, 1)
        quantize_w1(bf01, 0, 1, 1, 2)
        w1_raw[1, 1] = load_w1(1, 1, early_pass(0))
        round_w1(on_scalar, bf01, 0, 1, 2)
        round_w1(on_scalar, bf01, 0, 1, 3)
        gm_sb[1] = load_dealt(gm, 1, early_pass(1))
        pair = picked_pair(M)
        pick(pair, h[0], 0, 0, 0, M)
        quantize_w1(bf01, 0, 1, 2, 4)
        h[1] = first_stage(0, 1)
        bf10 = w1_staging(0)
        for t in range(4):
            round_w1(on_scalar, bf10, 1, 0, t)
        w3_raw0 = load_dealt(w3, 0, one_pass(1))
        h[2] = first_stage(0, 2)
        bf11 = w1_staging(10)
        for t in range(4):
            round_w1(on_scalar, bf11, 1, 1, t)
        pick(pair, h[1], 0, 1, 0, M)
        quantize_w1(bf10, 1, 0, 0, 4)
        h[3] = first_stage(0, 3)
        deal_w2_codes(1)
        quantize_w1(bf11, 1, 1, 0, 4)
        bf30 = round_w3(w3_raw0, 1)
        w3_raw1 = load_dealt(w3, 1, one_pass(1))
        pick(pair, h[2], 0, 2, 0, M)
        h[4] = first_stage(1, 0)
        bf31 = round_w3(w3_raw1, 2)
        pick(pair, h[3], 0, 3, 0, M)
        h[5] = first_stage(1, 1)
        z = meet(pair, M)
        h[6] = first_stage(1, 2)
        quantize_z(z, 0, 0, M)
        quantize_w3(bf30, 0)
        h[7] = first_stage(1, 3)
        quantize_w3(bf31, 1)

        banks = {}
        for lo in range(0, M, CHUNK):
            tag, bufs = ("y2", 2) if lo == 0 else ("y1", 6)
            banks[lo] = [psum.tile([P, BANK], F32, name="y", tag=tag, bufs=bufs) for i in range(2)]
            second_stage_pass(banks[lo], 0, lo, lo + CHUNK)
        for lo in range(0, M, CHUNK):
            pair = picked_pair(CHUNK)
            for t in range(4):
                pick(pair, h[4 + t], 1, t, lo, lo + CHUNK)
            z = meet(pair, CHUNK)
            quantize_z(z, 1, lo, lo + CHUNK)
            second_stage_pass(banks[lo], 1, lo, lo + CHUNK)
            finish(banks[lo], lo, lo + CHUNK)
